import numpy as np
CORES = [144,200,272,328,400,456]
N = 6
T, FF, CAP, CAPP = 2048, 4, 576, 192
def entries(a): return a.T.reshape(-1)
def pack(v, P): return np.ascontiguousarray(np.asarray(v, np.int32).reshape(-1, P).T)
def lists(rng, how):
    O = np.stack([rng.permutation(np.repeat(np.arange(N), CAPP))[:CAP] for k in range(N)])
    if how == "apart": s = int(rng.integers(N * CAPP - CAP + 1)); cnt = np.bincount(np.repeat(np.arange(N), CAPP)[s:s + CAP], minlength=N); a = rng.permutation(N); O = np.stack([rng.permutation(np.repeat(np.arange(N), cnt[(a + k) % N])) for k in rng.permutation(N)])
    if how == "full": z = rng.permutation(N); O = np.stack([rng.permutation(np.repeat(z, CAPP)[:CAP]) for k in range(N)])
    if how == "none": z = int(rng.integers(N)); O = np.stack([rng.permutation(np.repeat(np.delete(np.arange(N), z), CAPP))[:CAP] for k in range(N)])
    P = np.zeros((N, CAP), np.int64)
    for o in range(N):
        q = rng.permutation(T); u = 0
        for k in range(N):
            m = np.nonzero(O[k] == o)[0]
            if how != "apart": q = rng.permutation(T); u = 0
            if how == "sorted": q = np.r_[0, T - 1, 1 + rng.permutation(T - 2)]
            P[k, m] = T * o + q[u:u + len(m)]; u += len(m)
    if how == "same": P = np.stack([rng.permutation(P[0]) for k in range(N)])
    if how == "sorted": P = np.sort(P, axis=1)
    G = 2 * rng.random((N, 16, CAP // 16), dtype=np.float32) - 1
    if how == "none": G[rng.random(G.shape) < 0.125] = 0
    return {"gate": G, "pick": np.stack([pack(p, 16) for p in P])}
def setup_inputs(rng):
    return dict({"x": rng.standard_normal((N, 128, T), dtype=np.float32), "w1": (rng.standard_normal((N, 128, FF * 128), dtype=np.float32) / 8), "w2": (rng.standard_normal((N, 128, FF * 128), dtype=np.float32) / 16)}, **lists(rng, "uniform"))
def setup_inputs_apart(rng):
    d = setup_inputs(rng); d.update(lists(rng, "apart"))
    for k in ("x",): d[k] = (d[k].astype(np.float32) * 1024.0).astype(d[k].dtype)
    return d
def setup_inputs_full(rng):
    d = setup_inputs(rng); d.update(lists(rng, "full"))
    for k in ("x",): d[k] = (d[k].astype(np.float32) * (1 / 1024.0)).astype(d[k].dtype)
    return d
def setup_inputs_none(rng):
    d = setup_inputs(rng); d.update(lists(rng, "none"))
    return d
def setup_inputs_same(rng):
    d = setup_inputs(rng); d.update(lists(rng, "same"))
    return d
def setup_inputs_sorted(rng):
    d = setup_inputs(rng); d.update(lists(rng, "sorted"))
    return d
def check_inputs(x):
    bad = []
    if x["pick"].min() < 0 or x["pick"].max() >= N * T: bad.append("pick out of range")
    if any(len(np.unique(a)) != a.size for a in x["pick"]): bad.append("a token stands twice in a list")
    if max(int(np.bincount(entries(a) // T, minlength=N).max()) for a in x["pick"]) > CAPP: bad.append("more than CAPP of an expert's tokens lie on one rank")
    return bad
def reference(x, w1, w2, gate, pick):
    X, W1, W2 = x.astype(np.float64), w1.astype(np.float64), w2.astype(np.float64)
    A = np.concatenate(list(X), axis=1); Y = np.zeros((128, N * T))
    for k in range(N):
        P = entries(pick[k]); g = entries(gate[k]).astype(np.float64)
        Y[:, P] += g[None, :] * sum(W2[k][:, 128 * f:128 * f + 128].T @ np.maximum(W1[k][:, 128 * f:128 * f + 128].T @ A[:, P], 0.0) for f in range(FF))
    return {"y": np.stack([Y[:, T * r:T * r + T] for r in range(N)]).astype(np.float32)}

@@ -1,0 +1,386 @@
+from concourse.bass import DstId, RemoteDMATransfer
+from concourse.mybir import AluOpType, ActivationFunctionType
+
+TOK, FF, CAP, CAPP = 2048, 4, 576, 192
+WIN = TOK + CAPP
+RW, CH = 96, 6
+LC = CAPP // 16
+NEV = 128
+
+SCRATCH = {
+    "picki": ("sbuf", [128, 6], "int32"), "own": ("sbuf", [128, 6], "int32"), "slot": ("sbuf", [128, 6], "int32"),
+    "hl": ("sbuf", [128, 12], "int32"), "hlf": ("sbuf", [128, 12], "float32"), "uu": ("sbuf", [128, 6], "float32"),
+    "uw": ("sbuf", [128, 6], "float32"), "vv": ("sbuf", [128, 6], "float32"),
+    "pg": ("sbuf", [128, 16], "float32"), "wa": ("sbuf", [128, 512], "float32"), "wb": ("sbuf", [128, 512], "float32"),
+    "lt": ("sbuf", [128, 72], "uint16"), "ls": ("sbuf", [128, 432], "uint16"),
+    "mk": ("sbuf", [128, 36], "bfloat16"), "cu": ("sbuf", [128, 36], "bfloat16"), "seg": ("sbuf", [128, 36], "float32"),
+    "segb": ("sbuf", [128, 36], "bfloat16"),
+    "sm": ("sbuf", [128, 36], "float32"), "s18": ("sbuf", [128, 18], "float32"), "s6": ("sbuf", [128, 6], "float32"),
+    "neg": ("sbuf", [128, 96], "bfloat16"), "tri": ("sbuf", [128, 96], "bfloat16"), "oneb": ("sbuf", [128, 96], "bfloat16"),
+    "onef": ("sbuf", [128, 128], "float32"), "it": ("sbuf", [128, 192], "float32"), "im": ("sbuf", [128, 128], "float32"),
+    "c16": ("sbuf", [128, 72], "float32"), "kc": ("sbuf", [128, 36], "float32"),
+    "ohr": ("sbuf", [128, 432], "float32"), "ohl": ("sbuf", [128, 768], "float32"), "ohg": ("sbuf", [128, 1152], "float32"),
+    "ga": ("sbuf", [128, 6], "float32"), "gb": ("sbuf", [128, 6], "float32"), "gm": ("sbuf", [128, 6], "bfloat16"),
+    "gc6": ("sbuf", [128, 6], "bfloat16"), "gs": ("sbuf", [128, 18], "float32"), "gt": ("sbuf", [128, 192], "float32"),
+    "xw": ("sbuf", [128, WIN], "float32"), "yw": ("sbuf", [128, WIN], "float32"),
+    "gx": ("sbuf", [128, 1152], "float32"), "tk": ("sbuf", [128, 192], "float32"), "res": ("sbuf", [128, 1152], "float32"),
+    "tmp": ("sbuf", [128, 1152], "float32"), "hid": ("sbuf", [128, 768], "float32"), "ot": ("sbuf", [128, 192], "float32"),
+    "hp0": ("psum", [128, 512], "float32"), "hp1": ("psum", [128, 512], "float32"), "hp2": ("psum", [128, 512], "float32"),
+    "hp3": ("psum", [128, 512], "float32"), "op": ("psum", [128, 512], "float32"), "gp": ("psum", [128, 512], "float32"),
+    "rk": ("psum", [128, 512], "float32"), "lp": ("psum", [128, 512], "float32"),
+}
+SEMAPHORES = (["rPG", "rP1", "rP2", "rLT", "rTK"] + ["rLS%d" % k for k in range(6)] + ["rRS%d" % k for k in range(6)]
+              + ["e%d" % i for i in range(NEV)])
+PLAN = {}
+
+
+def engines(mask):
+    return [i for i in range(16) if (mask >> i) & 1]
+
+
+def make_plan(T, topo):
+    R = list(T.cores)
+    n = len(R)
+    H = [topo.host(c) for c in R]
+    C = [topo.chip(c) for c in R]
+    at = {}
+    for c in range(512):
+        at.setdefault((topo.host(c), topo.chip(c)), []).append(c)
+    numbers = sorted(set(C))
+
+    def other(ch):
+        return [z for z in numbers if z != ch][0]
+
+    def linked(a, b):
+        return topo.may_write(at[(a, C[0])][0], at[(b, C[0])][0])
+
+    def ports(h, ch):
+        return [c for c in at[(h, ch)] if topo.may_write(c, at[(h, other(ch))][0])]
+
+    def plain(h, ch):
+        return [c for c in at[(h, ch)] if c not in ports(h, ch) and c not in R]
+
+    rank_at = {(H[r], C[r]): r for r in range(n)}
+    mid = [h for h in range(4) if h not in H]
+    pair, where = {}, {}
+
+    def put(k, o, core):
+        pair[core] = (k, o)
+        where[(k, o)] = core
+
+    sends, arr = {}, {}
+
+    def send(src, key, items):
+        for d, db, d0, d1, sb, s0, s1, sem, eng in items:
+            arr[(d, sem)] = arr.get((d, sem), 0) + len(eng)
+        sends.setdefault(src, []).append((key, items))
+
+    def eng(core, d, what):
+        h, ch = topo.host(core), topo.chip(core)
+        mates_on = [c for c in at[(h, ch)] if c != core]
+        same = [c for c in range(512) if topo.same_plane(core, c)][0]
+        on, off = engines(topo.mask(core, mates_on[0])), engines(topo.mask(core, same))
+        up = [e for e in on if e not in off]
+        a = len(off) // 2
+        return {"off": off, "up": up, "lo": off[:a], "hi": off[a:], "up1": up[:len(up) // 2], "up2": up[len(up) // 2:],
+                "all": engines(topo.mask(core, d))}[what]
+
+    def PG(src, d, what):
+        return (d, "pg", 0, 16, "pg", 0, 16, "rPG", eng(src, d, what))
+
+    def P1(src, d, what):
+        return (d, "wa", 0, 512, "wa", 0, 512, "rP1", eng(src, d, what))
+
+    def P2(src, d, what):
+        return (d, "wb", 0, 512, "wb", 0, 512, "rP2", eng(src, d, what))
+
+    def LR(src, d, what):
+        return (d, "lt", 0, 72, "lt", 0, 72, "rLT", eng(src, d, what))
+
+    def LS(src, o, k, what):
+        return (R[o], "ls", 72 * k, 72 * k + 72, "lt", 0, 72, "rLS%d" % k, eng(src, R[o], what))
+
+    near = {k: [o for o in range(n) if H[o] == H[k] or linked(H[k], H[o])] for k in range(n)}
+    far_hosts = sorted(set(H[k] for k in range(n) if len(near[k]) < n))
+    for k in range(n):
+        h, ch = H[k], C[k]
+        P = ports(h, ch)
+        put(k, k, R[k])
+        for i, o in enumerate([o for o in near[k] if C[o] == ch and o != k]):
+            put(k, o, [P[0], P[2]][i])
+        r = rank_at[(h, other(ch))]
+        P, Q = ports(h, other(ch)), plain(h, other(ch))
+        for i, o in enumerate([r] + [o for o in near[k] if C[o] != ch and o != r]):
+            put(k, o, [Q[0], Q[1], P[1]][i])
+        far = [o for o in range(n) if o not in near[k]]
+        if far:
+            m = [z for z in mid if linked(z, h) and linked(z, H[far[0]])][0]
+            i = far_hosts.index(h)
+            for o in far:
+                P = ports(m, C[o])
+                put(k, o, P[i] if C[o] == ch else P[2 + i])
+    for k in range(n):
+        h, ch, c0 = H[k], C[k], R[k]
+        P, Q = ports(h, ch), plain(h, ch)
+        A, B, L = P[0], P[2], P[3]
+        same = [o for o in near[k] if C[o] == ch and o != k]
+        cross = [o for o in near[k] if C[o] != ch]
+        cross = [o for o in cross if H[o] != h] + [o for o in cross if H[o] == h]
+        grp = [where[(k, o)] for o in cross[::-1]]
+        far = [o for o in range(n) if o not in near[k]]
+        X, Y = grp[0], grp[1]
+        Z = grp[2] if len(grp) > 2 else None
+        if far:
+            rl = where[(k, [o for o in far if C[o] == ch][0])]
+            lf = where[(k, [o for o in far if C[o] != ch][0])]
+            D = Q[2]
+            send(c0, "pg", [PG(c0, L, "up"), PG(c0, rl, "off")])
+            send(c0, "w1", [P1(c0, A, "off"), P1(c0, D, "up")])
+            send(c0, "w2", [P2(c0, B, "up")])
+            send(c0, "lt", [LR(c0, L, "lo"), LR(c0, rl, "hi")])
+            send(c0, "lt", [LS(c0, same[0], k, "off")])
+            send(L, "rPG", [PG(L, X, "off"), PG(L, A, "up")])
+            send(L, "rLT", [LS(L, cross[0], k, "lo"), LS(L, cross[1], k, "hi")])
+            send(A, "rP1", [P1(A, X, "lo"), P1(A, lf, "hi")])
+            send(B, "rP2", [P2(B, Y, "lo"), P2(B, lf, "hi"), P2(B, A, "up")])
+            send(D, "rP1", [P1(D, rl, "off")])
+            send(rl, "rPG", [PG(rl, lf, "off")])
+            send(rl, "rLT", [LS(rl, far[0], k, "lo"), LS(rl, far[1], k, "hi")])
+            send(lf, "rP2", [P2(lf, rl, "off")])
+        else:
+            send(c0, "pg", [PG(c0, L, "off")])
+            send(c0, "w1", [P1(c0, A, "all")])
+            send(c0, "w2", [P2(c0, B, "up")])
+            send(c0, "lt", [LR(c0, L, "off")])
+            send(c0, "lt", [LS(c0, same[0], k, "lo"), LS(c0, same[1], k, "hi")])
+            send(L, "rPG", [PG(L, Z, "off"), PG(L, A, "up1"), PG(L, B, "up2")])
+            send(L, "rLT", [LS(L, cross[0], k, "lo"), LS(L, cross[1], k, "hi")])
+            send(L, "rLT", [LS(L, cross[2], k, "off")])
+            send(A, "rP1", [P1(A, X, "off"), P1(A, B, "up")])
+            send(B, "rP2", [P2(B, Y, "off"), P2(B, A, "up")])
+        if Z is None:
+            send(X, "rPG", [PG(X, Y, "all")])
+            send(X, "rP1", [P1(X, Y, "all")])
+            send(Y, "rP2", [P2(Y, X, "all")])
+        else:
+            send(Z, "rPG", [PG(Z, X, "off"), PG(Z, Y, "up")])
+            send(X, "rP1", [P1(X, Y, "off"), P1(X, Z, "up")])
+            send(Y, "rP2", [P2(Y, X, "off"), P2(Y, Z, "up")])
+    order, back = {}, {}
+    for o in range(n):
+        def key(k, o=o):
+            if k == o:
+                return 9
+            if H[k] == H[o]:
+                return 5
+            if o not in near[k]:
+                return 3
+            return 1 if C[k] == C[o] else 2
+        order[o] = sorted(range(n), key=key)
+        back[o] = [o] + [k for k in order[o] if H[k] == H[o] and k != o] + [k for k in order[o] if H[k] != H[o]]
+        for k in order[o][:-1]:
+            d = where[(k, o)]
+            hd = topo.host(d)
+            what = "up" if hd == H[o] else ("lo" if topo.rack(hd) != topo.rack(H[o]) else "hi")
+            send(R[o], "gx%d" % k, [(d, "tk", 0, 192, "gx", 192 * k, 192 * k + 192, "rTK", eng(R[o], d, what))])
+    for (k, o), c in where.items():
+        if c != R[o]:
+            send(c, "ot", [(R[o], "res", 192 * k, 192 * k + 192, "ot", 0, 192, "rRS%d" % k, eng(c, R[o], "all"))])
+    return {"pair": pair, "sends": sends, "arr": arr, "order": order, "back": back}
+
+
+def rank_program(g, core, T, topo):
+    if "p" not in PLAN:
+        PLAN["p"] = make_plan(T, topo)
+    plan = PLAN["p"]
+    if core not in plan["sends"]:
+        return
+    me = T.rank_of(core)
+    V, PE, S, SY = g.vector, g.tensor, g.scalar, g.sync
+    cnt, evs, waited, seen = {}, {}, set(), set()
+
+    def new():
+        name = "e%d" % len(cnt)
+        cnt[name] = 0
+        return name
+
+    def wait(q, qn, deps):
+        for d in deps:
+            if d is None or (qn, d) in seen:
+                continue
+            seen.add((qn, d))
+            waited.add(d)
+            q.wait_ge(T.sem[d], cnt[d] if d in cnt else plan["arr"][(core, d)])
+
+    def done(instr, ev=None, k=1):
+        ev = ev or new()
+        instr.then_inc(T.sem[ev], k)
+        cnt[ev] += k
+        return ev
+
+    def vec(deps):
+        wait(V, "v", deps)
+        return V
+
+    def pe(deps):
+        wait(PE, "p", deps)
+        return PE
+
+    def sc(deps):
+        wait(S, "s", deps)
+        return S
+
+    EQ, MUL, ADD, SUB, MAX = AluOpType.is_equal, AluOpType.mult, AluOpType.add, AluOpType.subtract, AluOpType.max
+    compute = core in plan["pair"]
+    xgate = new()
+    if me is not None:
+        cnt[xgate] = 1
+
+    if me is not None:
+        ld_pick = done(SY.dma_start(T.picki[0:RW, :], T.pick[:, :]), None, 16)
+        ld_w1 = done(SY.dma_start(T.wa[:, :], T.w1[:, :]), None, 16)
+        pg0 = done(V.memset(T.pg[:, :], 0.0))
+        wait(S, "s", [pg0])
+        ld_gate = done(S.dma_start(T.pg[0:RW, 8:14], T.gate[:, :]), None, 16)
+        ld_w2 = done(S.dma_start(T.wb[:, :], T.w2[:, :]), None, 16)
+        ld_x1 = done(SY.dma_start(T.xw[:, CAPP:CAPP + TOK // 2], T.x[:, 0:TOK // 2]), None, 16)
+        wait(SY, "y", [xgate])
+        ld_x2 = done(SY.dma_start(T.xw[:, CAPP + TOK // 2:WIN], T.x[:, TOK // 2:TOK]), None, 16)
+        evs["w1"], evs["w2"] = [ld_w1], [ld_w2]
+
+    if compute:
+        c_neg = done(V.memset(T.neg[0:RW, :], -1.0))
+        c_one = done(V.memset(T.oneb[0:RW, :], 1.0))
+        c_onf = done(V.memset(T.onef[0:RW, :], 1.0))
+        wait(g, "g", [c_neg])
+        c_tri = done(g.affine_select(T.tri[0:RW, :], T.neg[0:RW, :], [[-1, RW]], AluOpType.is_ge, 0.0, 0, 1))
+        if me is not None:
+            c_seg = done(g.iota(T.seg[0:RW, :], [[0, 6], [1, 6]], 0, 0, allow_small_or_imprecise_dtypes=True))
+            c_kc = done(g.iota(T.kc[0:1, :], [[CAPP, 6], [0, 6]], 0, 0, allow_small_or_imprecise_dtypes=True))
+            c_im = done(g.iota(T.im[0:RW, :], [[0, 8], [1, 16]], 0, 0, allow_small_or_imprecise_dtypes=True))
+            c_c16 = done(g.iota(T.c16[0:1, :], [[0, 6], [16, LC]], 0, 0, allow_small_or_imprecise_dtypes=True))
+        c_it = done(g.iota(T.it[0:RW, :], [[1, CAPP]], 0, 0, allow_small_or_imprecise_dtypes=True))
+
+    if me is not None:
+        x0 = done(V.memset(T.xw[:, 0:CAPP], 0.0))
+        y0 = done(V.memset(T.yw[:, 0:WIN // 2], 0.0))
+        c_segb = done(vec([c_seg]).tensor_scalar(T.segb[0:RW, :], T.seg[0:RW, :], 1.0, None, AluOpType.min))
+        e_lp = done(pe([c_onf, c_im, c_c16]).matmul(T.lp[:, 0:72], T.onef[0:1, :], T.c16[0:1, :], True, False))
+        done(PE.matmul(T.lp[:, 0:72], T.im[0:1, :], T.onef[0:1, 0:72], False, False), e_lp)
+        e_rk = done(pe([c_kc]).matmul(T.rk[0:RW, 0:36], T.onef[0:1, 0:RW], T.kc[0:1, :], True, False))
+        e_own = done(vec([ld_pick]).tensor_scalar(T.own[0:RW, :], T.picki[0:RW, :], 11, None, AluOpType.arith_shift_right))
+        e_pf = done(vec([pg0]).tensor_copy(T.pg[0:RW, 0:6], T.picki[0:RW, :]))
+        evs["pg"] = [e_pf, ld_gate]
+        e_mk = None
+        for o in range(6):
+            e_mk = done(vec([e_own]).tensor_scalar(T.mk[0:RW, 6 * o:6 * o + 6], T.own[0:RW, :], float(o), None, EQ), e_mk)
+        done(pe([e_mk, c_tri]).matmul(T.rk[0:RW, 0:36], T.tri[0:RW, :], T.mk[0:RW, :], False, False), e_rk)
+        e_cu = done(vec([e_mk, c_segb]).tensor_tensor_scan(T.cu[0:RW, :], T.segb[0:RW, :], T.mk[0:RW, :], 0.0, MUL, ADD))
+        done(pe([e_cu, c_one]).matmul(T.rk[0:RW, 0:36], T.oneb[0:RW, :], T.cu[0:RW, :], False, True), e_rk)
+        e_uw = done(vec([]).tensor_scalar(T.uw[0:RW, :], T.own[0:RW, :], float(CAPP - TOK), float(CAPP), MUL, ADD))
+        e_uu = done(vec([e_uw]).tensor_tensor(T.uu[0:RW, :], T.uw[0:RW, :], T.picki[0:RW, :], ADD))
+        e_sm = done(vec([e_rk]).tensor_tensor(T.sm[0:RW, :], T.rk[0:RW, 0:36], T.mk[0:RW, :], MUL))
+        e_s18 = done(vec([e_sm]).tensor_tensor(T.s18[0:RW, :], T.sm[0:RW, 0:18], T.sm[0:RW, 18:36], ADD))
+        e_s6 = done(vec([e_s18]).tensor_tensor(T.s6[0:RW, :], T.s18[0:RW, 0:6], T.s18[0:RW, 6:12], ADD))
+        e_sl = done(vec([e_s6]).tensor_tensor(T.slot[0:RW, :], T.s6[0:RW, :], T.s18[0:RW, 12:18], ADD))
+        e_hl = done(vec([e_sl]).tensor_scalar(T.hl[0:RW, 0:6], T.slot[0:RW, :], 4, None, AluOpType.arith_shift_right))
+        done(V.tensor_scalar(T.hl[0:RW, 6:12], T.slot[0:RW, :], 15, None, AluOpType.bitwise_and), e_hl)
+        e_vv = done(vec([e_uu]).tensor_tensor(T.vv[0:RW, :], T.uu[0:RW, :], T.slot[0:RW, :], SUB))
+        e_hf = done(vec([e_hl]).tensor_copy(T.hlf[0:RW, :], T.hl[0:RW, :]))
+        vec([e_hf, e_vv, c_it, c_im])
+        for c in range(CH):
+            e_oh = done(V.tensor_scalar(T.ohr[0:RW, 72 * c:72 * c + 72], T.it[0:RW, 0:72], T.hlf[0:RW, c:c + 1],
+                                        T.vv[0:RW, c:c + 1], EQ, MUL))
+            done(V.tensor_scalar(T.ohl[0:RW, 128 * c:128 * c + 128], T.im[0:RW, :], T.hlf[0:RW, 6 + c:7 + c], None, EQ), e_oh)
+            done(pe([e_oh]).matmul(T.lp[:, 0:72], T.ohl[0:RW, 128 * c:128 * c + 128], T.ohr[0:RW, 72 * c:72 * c + 72],
+                                   False, c == CH - 1), e_lp)
+        e_lt = done(vec([e_lp]).tensor_copy(T.lt[:, :], T.lp[:, 0:72]))
+        evs["lt"] = [e_lt]
+        done(V.memset(T.yw[:, WIN // 2:WIN], 0.0), y0)
+
+    def gate_first(k, o, deps):
+        a = done(vec(deps).tensor_scalar(T.ga[0:RW, :], T.pg[0:RW, 0:6], float(TOK * o), None, AluOpType.is_ge))
+        done(V.tensor_scalar(T.gb[0:RW, :], T.pg[0:RW, 0:6], float(TOK * o + TOK), None, AluOpType.is_lt), a)
+        b = done(vec([a]).tensor_tensor(T.gm[0:RW, :], T.ga[0:RW, :], T.gb[0:RW, :], MUL))
+        c = done(vec([b, c_one]).tensor_tensor_scan(T.gc6[0:RW, :], T.oneb[0:RW, 0:6], T.gm[0:RW, :], 0.0, MUL, ADD))
+        r = done(pe([b, c_tri]).matmul(T.gp[0:RW, 0:6], T.tri[0:RW, :], T.gm[0:RW, :], True, False))
+        done(pe([c, c_one]).matmul(T.gp[0:RW, 0:6], T.oneb[0:RW, :], T.gc6[0:RW, :], False, True), r)
+        s = done(vec([r]).tensor_scalar(T.gs[0:RW, 0:6], T.gp[0:RW, 0:6], 1.0, None, ADD))
+        t = done(vec([s]).tensor_tensor(T.gs[0:RW, 6:12], T.gs[0:RW, 0:6], T.gm[0:RW, :], MUL))
+        u = done(vec([t]).tensor_scalar(T.gs[0:RW, 12:18], T.gs[0:RW, 6:12], 1.0, None, SUB))
+        vec([u, c_it])
+        h = None
+        for c in range(CH):
+            h = done(V.tensor_scalar(T.ohg[0:RW, 192 * c:192 * c + 192], T.it[0:RW, :], T.gs[0:RW, 12 + c:13 + c],
+                                     T.pg[0:RW, 8 + c:9 + c], EQ, MUL), h)
+        m = None
+        for c in range(CH):
+            m = done(pe([h, c_onf]).matmul(T.gp[:, 0:192], T.onef[0:RW, :], T.ohg[0:RW, 192 * c:192 * c + 192],
+                                           c == 0, c == CH - 1), m)
+        return m
+
+    def layers(tok, tdeps, d1, d2, both):
+        H = [T.hp0, T.hp1, T.hp2, T.hp3]
+        a = [done(pe(tdeps + d1).matmul(H[f][:, 0:192], T.wa[:, 128 * f:128 * f + 128], tok, True, True)) for f in range(FF)]
+        m = None
+        for f in range(FF):
+            hid = T.hid[:, 192 * f:192 * f + 192]
+            if both and f % 2 == 0:
+                r = done(vec([a[f]]).tensor_scalar(hid, H[f][:, 0:192], 0.0, None, MAX))
+            else:
+                r = done(sc([a[f]]).activation(hid, H[f][:, 0:192], ActivationFunctionType.Relu))
+            m = done(pe(d2 + [r]).matmul(T.op[:, 0:192], T.wb[:, 128 * f:128 * f + 128], hid, f == 0, f == FF - 1), m)
+        return m
+
+    if compute:
+        k, o = plan["pair"][core]
+    if compute and me is None:
+        gm = gate_first(k, o, ["rPG"])
+        gt = done(vec([gm]).tensor_copy(T.gt[:, :], T.gp[:, 0:192]))
+        m = layers(T.tk[:, :], ["rTK"], ["rP1"], ["rP2"], True)
+        evs["ot"] = [done(vec([m, gt]).tensor_tensor(T.ot[:, :], T.op[:, 0:192], T.gt[:, :], MUL))]
+
+    if me is not None:
+        gm = gate_first(k, o, [e_pf, ld_gate])
+        vec([x0, ld_x1, ld_x2])
+
+        def off(k):
+            return T.lt[:, LC * me:LC * me + LC] if k == me else T.ls[:, 72 * k + LC * me:72 * k + LC * me + LC]
+
+        for k in plan["order"][me]:
+            dep = [e_lt] if k == me else ["rLS%d" % k]
+            evs["gx%d" % k] = [done(vec(dep).tensor_copy(T.gx[:, 192 * k:192 * k + 192], T.xw[:, :].indirect(off(k))))]
+        gt = done(vec([gm]).tensor_copy(T.gt[:, :], T.gp[:, 0:192]))
+        m = layers(T.gx[:, 192 * me:192 * me + 192], evs["gx%d" % me], [ld_w1], [ld_w2], False)
+        last = done(vec([m, gt]).tensor_tensor(T.ot[:, :], T.op[:, 0:192], T.gt[:, :], MUL))
+        last = done(vec([last, y0]).tensor_copy(T.yw[:, :].indirect(off(me)), T.ot[:, :]))
+        for k in plan["back"][me][1:]:
+            t = T.tmp[:, 192 * k:192 * k + 192]
+            a = done(vec(["rRS%d" % k, last]).tensor_tensor(t, T.yw[:, :].indirect(off(k)), T.res[:, 192 * k:192 * k + 192], ADD))
+            last = done(vec([a]).tensor_copy(T.yw[:, :].indirect(off(k)), t))
+        wait(SY, "y", [last])
+        done(SY.dma_start(T.y[:, 0:TOK // 2], T.yw[:, CAPP:CAPP + TOK // 2]), None, 16)
+        wait(S, "s", [last])
+        done(S.dma_start(T.y[:, TOK // 2:TOK], T.yw[:, CAPP + TOK // 2:WIN]), None, 16)
+
+    steps = plan["sends"][core]
+    for i, (key, items) in enumerate(steps):
+        wait(g, "g", evs[key] if key in evs else [key])
+        ev = new()
+        cnt[ev] = sum(len(t[8]) for t in items)
+        masks = [sum(1 << e for e in t[8]) for t in items]
+        if len(items) == 1:
+            d, db, d0, d1, sb, s0, s1, sem, eng = items[0]
+            rid, pid = topo.addr(d, core)
+            g.remote_dma(T[db][:, d0:d1], T[sb][:, s0:s1], T.sem[sem], T.sem[ev], pid, rid, masks[0])
+        else:
+            tr = []
+            for (d, db, d0, d1, sb, s0, s1, sem, eng), mk in zip(items, masks):
+                rid, pid = topo.addr(d, core)
+                tr.append(RemoteDMATransfer(dst_ids=[DstId(rid=rid, pnc=pid)], dma_engine_mask=mk, remote_sem=T.sem[sem],
+                                            src=T[sb][:, s0:s1], dst=T[db][:, d0:d1]))
+            g.remote_dma_fused(tr, local_sem=T.sem[ev])
+        if me is not None and key == "lt" and steps[i + 1][0] != "lt":
+            g.sem_inc(T.sem[xgate], 1)
+    wait(g, "g", [e for e in cnt if e not in waited and cnt[e]])
+    wait(g, "g", [s for (c, s) in plan["arr"] if c == core and s not in waited])

@@ -1,21 +1,20 @@
 from concourse.bass import DstId, RemoteDMATransfer
-from concourse.mybir import AluOpType, ActivationFunctionType
+from concourse.mybir import AluOpType, AxisListType, ActivationFunctionType
 
 TOK, FF, CAP, CAPP = 2048, 4, 576, 192
 WIN = TOK + CAPP
 RW, CH = 96, 6
 LC = CAPP // 16
-NEV = 128
+NEV = 120
 
 SCRATCH = {
     "picki": ("sbuf", [128, 6], "int32"), "own": ("sbuf", [128, 6], "int32"), "slot": ("sbuf", [128, 6], "int32"),
     "hl": ("sbuf", [128, 12], "int32"), "hlf": ("sbuf", [128, 12], "float32"), "uu": ("sbuf", [128, 6], "float32"),
-    "uw": ("sbuf", [128, 6], "float32"), "vv": ("sbuf", [128, 6], "float32"),
-    "pg": ("sbuf", [128, 16], "float32"), "wa": ("sbuf", [128, 512], "float32"), "wb": ("sbuf", [128, 512], "float32"),
+    "uw": ("sbuf", [128, 6], "float32"), "vv": ("sbuf", [128, 6], "float32"), "gin": ("sbuf", [128, 6], "float32"),
+    "pg": ("sbuf", [128, 12], "float32"), "ww": ("sbuf", [128, 1024], "float32"), "fw": ("sbuf", [128, 256], "float32"),
     "lt": ("sbuf", [128, 72], "uint16"), "ls": ("sbuf", [128, 432], "uint16"),
     "mk": ("sbuf", [128, 36], "bfloat16"), "cu": ("sbuf", [128, 36], "bfloat16"), "seg": ("sbuf", [128, 36], "float32"),
-    "segb": ("sbuf", [128, 36], "bfloat16"),
-    "sm": ("sbuf", [128, 36], "float32"), "s18": ("sbuf", [128, 18], "float32"), "s6": ("sbuf", [128, 6], "float32"),
+    "segb": ("sbuf", [128, 36], "bfloat16"), "sm": ("sbuf", [128, 36], "float32"),
     "neg": ("sbuf", [128, 96], "bfloat16"), "tri": ("sbuf", [128, 96], "bfloat16"), "oneb": ("sbuf", [128, 96], "bfloat16"),
     "onef": ("sbuf", [128, 128], "float32"), "it": ("sbuf", [128, 192], "float32"), "im": ("sbuf", [128, 128], "float32"),
     "c16": ("sbuf", [128, 72], "float32"), "kc": ("sbuf", [128, 36], "float32"),
@@ -29,8 +28,8 @@ SCRATCH = {
     "hp3": ("psum", [128, 512], "float32"), "op": ("psum", [128, 512], "float32"), "gp": ("psum", [128, 512], "float32"),
     "rk": ("psum", [128, 512], "float32"), "lp": ("psum", [128, 512], "float32"),
 }
-SEMAPHORES = (["rPG", "rP1", "rP2", "rLT", "rTK"] + ["rLS%d" % k for k in range(6)] + ["rRS%d" % k for k in range(6)]
-              + ["e%d" % i for i in range(NEV)])
+SEMAPHORES = (["rG", "rGa", "rGb", "rW0", "rW1", "rW2", "rW3", "rFW", "rLT", "rTK"] + ["rLS%d" % k for k in range(6)]
+              + ["rRS%d" % k for k in range(6)] + ["e%d" % i for i in range(NEV)])
 PLAN = {}
 
 
@@ -54,6 +53,9 @@ def make_plan(T, topo):
     def linked(a, b):
         return topo.may_write(at[(a, C[0])][0], at[(b, C[0])][0])
 
+    def cabled(h):
+        return [z for z in range(4) if topo.rack(z) != topo.rack(h) and linked(h, z)][0]
+
     def ports(h, ch):
         return [c for c in at[(h, ch)] if topo.may_write(c, at[(h, other(ch))][0])]
 
@@ -61,38 +63,45 @@ def make_plan(T, topo):
         return [c for c in at[(h, ch)] if c not in ports(h, ch) and c not in R]
 
     rank_at = {(H[r], C[r]): r for r in range(n)}
-    mid = [h for h in range(4) if h not in H]
+    mid = [h for h in range(4) if h not in H][0]
     pair, where = {}, {}
-
-    def put(k, o, core):
-        pair[core] = (k, o)
-        where[(k, o)] = core
-
     sends, arr = {}, {}
 
-    def send(src, key, items):
+    def send(src, prio, key, items):
         for d, db, d0, d1, sb, s0, s1, sem, eng in items:
             arr[(d, sem)] = arr.get((d, sem), 0) + len(eng)
-        sends.setdefault(src, []).append((key, items))
+        sends.setdefault(src, []).append((prio, key, items))
 
     def eng(core, d, what):
         h, ch = topo.host(core), topo.chip(core)
-        mates_on = [c for c in at[(h, ch)] if c != core]
+        near_core = [c for c in at[(h, ch)] if c != core][0]
         same = [c for c in range(512) if topo.same_plane(core, c)][0]
-        on, off = engines(topo.mask(core, mates_on[0])), engines(topo.mask(core, same))
+        on, off = engines(topo.mask(core, near_core)), engines(topo.mask(core, same))
         up = [e for e in on if e not in off]
-        a = len(off) // 2
-        return {"off": off, "up": up, "lo": off[:a], "hi": off[a:], "up1": up[:len(up) // 2], "up2": up[len(up) // 2:],
-                "all": engines(topo.mask(core, d))}[what]
+        a, b = len(off) // 2, len(off) // 4
+        return {"off": off, "up": up, "lo": off[:a], "hi": off[a:], "lo1": off[:b], "lo2": off[b:a], "hi1": off[a:a + b],
+                "hi2": off[a + b:], "up1": up[:len(up) // 2], "up2": up[len(up) // 2:], "all": engines(topo.mask(core, d))}[what]
 
-    def PG(src, d, what):
-        return (d, "pg", 0, 16, "pg", 0, 16, "rPG", eng(src, d, what))
+    def G(src, d, what):
+        return (d, "pg", 0, 12, "pg", 0, 12, "rG", eng(src, d, what))
 
-    def P1(src, d, what):
-        return (d, "wa", 0, 512, "wa", 0, 512, "rP1", eng(src, d, what))
+    def Ga(src, d, what):
+        return (d, "pg", 0, 6, "pg", 0, 6, "rGa", eng(src, d, what))
 
-    def P2(src, d, what):
-        return (d, "wb", 0, 512, "wb", 0, 512, "rP2", eng(src, d, what))
+    def Gb(src, d, what):
+        return (d, "pg", 6, 12, "pg", 6, 12, "rGb", eng(src, d, what))
+
+    def W(src, d, j, what):
+        return (d, "ww", 256 * j, 256 * j + 256, "ww", 256 * j, 256 * j + 256, "rW%d" % j, eng(src, d, what))
+
+    def W_fw(src, d, j, what):
+        return (d, "fw", 0, 256, "ww", 256 * j, 256 * j + 256, "rFW", eng(src, d, what))
+
+    def FW(src, d, j, what):
+        return (d, "ww", 256 * j, 256 * j + 256, "fw", 0, 256, "rW%d" % j, eng(src, d, what))
+
+    def FW_fw(src, d, what):
+        return (d, "fw", 0, 256, "fw", 0, 256, "rFW", eng(src, d, what))
 
     def LR(src, d, what):
         return (d, "lt", 0, 72, "lt", 0, 72, "rLT", eng(src, d, what))
@@ -101,91 +110,106 @@ def make_plan(T, topo):
         return (R[o], "ls", 72 * k, 72 * k + 72, "lt", 0, 72, "rLS%d" % k, eng(src, R[o], what))
 
     near = {k: [o for o in range(n) if H[o] == H[k] or linked(H[k], H[o])] for k in range(n)}
-    far_hosts = sorted(set(H[k] for k in range(n) if len(near[k]) < n))
     for k in range(n):
-        h, ch = H[k], C[k]
-        P = ports(h, ch)
-        put(k, k, R[k])
-        for i, o in enumerate([o for o in near[k] if C[o] == ch and o != k]):
-            put(k, o, [P[0], P[2]][i])
-        r = rank_at[(h, other(ch))]
-        P, Q = ports(h, other(ch)), plain(h, other(ch))
-        for i, o in enumerate([r] + [o for o in near[k] if C[o] != ch and o != r]):
-            put(k, o, [Q[0], Q[1], P[1]][i])
-        far = [o for o in range(n) if o not in near[k]]
-        if far:
-            m = [z for z in mid if linked(z, h) and linked(z, H[far[0]])][0]
-            i = far_hosts.index(h)
-            for o in far:
-                P = ports(m, C[o])
-                put(k, o, P[i] if C[o] == ch else P[2 + i])
+        for o in range(n):
+            h, ch = H[k], C[o]
+            if h == H[o]:
+                c = R[k] if C[k] == ch else plain(h, ch)[0]
+            elif topo.rack(h) == topo.rack(H[o]):
+                c = ports(h, ch)[1] if C[k] == ch else plain(h, ch)[1]
+            else:
+                t = H[o] if cabled(h) in H else cabled(h)
+                c = ports(t, ch)[0] if C[k] == ch else plain(t, ch)[-1]
+            pair[c] = (k, o)
+            where[(k, o)] = c
     for k in range(n):
         h, ch, c0 = H[k], C[k], R[k]
         P, Q = ports(h, ch), plain(h, ch)
-        A, B, L = P[0], P[2], P[3]
+        L, S = P[2], [Q[0], P[1], Q[2], P[3]]
         same = [o for o in near[k] if C[o] == ch and o != k]
         cross = [o for o in near[k] if C[o] != ch]
         cross = [o for o in cross if H[o] != h] + [o for o in cross if H[o] == h]
-        grp = [where[(k, o)] for o in cross[::-1]]
         far = [o for o in range(n) if o not in near[k]]
-        X, Y = grp[0], grp[1]
-        Z = grp[2] if len(grp) > 2 else None
+        mate_o = [o for o in range(n) if H[o] != h and topo.rack(H[o]) == topo.rack(h)]
+        X = where[(k, rank_at[(h, other(ch))])]
+        Y = [where[(k, o)] for o in mate_o if C[o] != ch]
+        O = [where[(k, o)] for o in mate_o if C[o] == ch]
+        rest = [o for o in range(n) if topo.rack(H[o]) != topo.rack(h)]
+        first = [o for o in rest if H[o] == cabled(h)] or rest
+        E = where[(k, [o for o in first if C[o] == ch][0])]
+        F = where[(k, [o for o in first if C[o] != ch][0])]
+        M, E2, F2 = [], None, None
+        PM, QM = ports(mid, ch), plain(mid, ch)
+        if far and first != rest:
+            M = [QM[0], PM[1], QM[-1], PM[3]]
+            E2 = where[(k, [o for o in far if C[o] == ch][0])]
+            F2 = where[(k, [o for o in far if C[o] != ch][0])]
+        rl = (M[1] if M else PM[2]) if far else None
+        it = [G(c0, L, "up1" if far and O else ("up" if far else "off"))]
+        it += [G(c0, z, "up2" if far else "up") for z in O]
+        it += [G(c0, rl, "off")] if far else []
+        send(c0, 0, "pg", it)
+        send(c0, 0, "w1", [W(c0, S[1], 0, "up1"), W(c0, S[1], 1, "up2"), W_fw(c0, S[0], 0, "hi")])
+        send(c0, 0, "w2", [W(c0, S[3], 2, "up1"), W(c0, S[3], 3, "up2"), W_fw(c0, S[2], 2, "hi")])
+        send(c0, 0, "lt", [LR(c0, L, "lo"), LR(c0, rl, "hi")] if far else [LR(c0, L, "off")])
+        send(c0, 0, "lt", [LS(c0, o, k, w) for o, w in zip(same, ["off"] if len(same) == 1 else ["lo", "hi"])])
+        if Y:
+            send(L, 0, "rG", [Ga(L, X, "lo"), Gb(L, Y[0], "hi")])
+            send(X, 0, "rGa", [Ga(X, Y[0], "all")])
+            send(Y[0], 0, "rGb", [Gb(Y[0], X, "all")])
+            if first != rest or not far:
+                send(L, 0, "rG", [G(L, E, "off")])
+        else:
+            send(L, 0, "rG", [G(L, X, "lo"), G(L, E, "hi")])
+        send(E, 0, "rG", [G(E, F, "off")])
         if far:
-            rl = where[(k, [o for o in far if C[o] == ch][0])]
-            lf = where[(k, [o for o in far if C[o] != ch][0])]
-            D = Q[2]
-            send(c0, "pg", [PG(c0, L, "up"), PG(c0, rl, "off")])
-            send(c0, "w1", [P1(c0, A, "off"), P1(c0, D, "up")])
-            send(c0, "w2", [P2(c0, B, "up")])
-            send(c0, "lt", [LR(c0, L, "lo"), LR(c0, rl, "hi")])
-            send(c0, "lt", [LS(c0, same[0], k, "off")])
-            send(L, "rPG", [PG(L, X, "off"), PG(L, A, "up")])
-            send(L, "rLT", [LS(L, cross[0], k, "lo"), LS(L, cross[1], k, "hi")])
-            send(A, "rP1", [P1(A, X, "lo"), P1(A, lf, "hi")])
-            send(B, "rP2", [P2(B, Y, "lo"), P2(B, lf, "hi"), P2(B, A, "up")])
-            send(D, "rP1", [P1(D, rl, "off")])
-            send(rl, "rPG", [PG(rl, lf, "off")])
-            send(rl, "rLT", [LS(rl, far[0], k, "lo"), LS(rl, far[1], k, "hi")])
-            send(lf, "rP2", [P2(lf, rl, "off")])
-        else:
-            send(c0, "pg", [PG(c0, L, "off")])
-            send(c0, "w1", [P1(c0, A, "all")])
-            send(c0, "w2", [P2(c0, B, "up")])
-            send(c0, "lt", [LR(c0, L, "off")])
-            send(c0, "lt", [LS(c0, same[0], k, "lo"), LS(c0, same[1], k, "hi")])
-            send(L, "rPG", [PG(L, Z, "off"), PG(L, A, "up1"), PG(L, B, "up2")])
-            send(L, "rLT", [LS(L, cross[0], k, "lo"), LS(L, cross[1], k, "hi")])
-            send(L, "rLT", [LS(L, cross[2], k, "off")])
-            send(A, "rP1", [P1(A, X, "off"), P1(A, B, "up")])
-            send(B, "rP2", [P2(B, Y, "off"), P2(B, A, "up")])
-        if Z is None:
-            send(X, "rPG", [PG(X, Y, "all")])
-            send(X, "rP1", [P1(X, Y, "all")])
-            send(Y, "rP2", [P2(Y, X, "all")])
-        else:
-            send(Z, "rPG", [PG(Z, X, "off"), PG(Z, Y, "up")])
-            send(X, "rP1", [P1(X, Y, "off"), P1(X, Z, "up")])
-            send(Y, "rP2", [P2(Y, X, "off"), P2(Y, Z, "up")])
+            z = E2 if M else E
+            send(rl, 0, "rG", [G(rl, z, "all")])
+            if M:
+                send(E2, 0, "rG", [G(E2, F2, "off")])
+        send(L, 1, "rLT", [LS(L, cross[0], k, "lo"), LS(L, cross[1], k, "hi")])
+        if cross[2:]:
+            send(L, 1, "rLT", [LS(L, cross[2], k, "off")])
+        if far:
+            send(rl, 1, "rLT", [LS(rl, far[0], k, "lo"), LS(rl, far[1], k, "hi")])
+        for j in (0, 2):
+            send(S[j], 2, "rFW", [FW(S[j], E, j, "lo"), FW_fw(S[j], M[j], "hi")] if M else [FW(S[j], E, j, "off")])
+        for j in (1, 3):
+            send(S[j], 2, "rW%d" % j, [W(S[j], E, j, "lo1"), W_fw(S[j], M[j], j, "lo2")] if M else [W(S[j], E, j, "lo")])
+            send(S[j], 3, ["rW%d" % (j - 1), "rW%d" % j], [W(S[j], X, j - 1, "hi1"), W(S[j], X, j, "hi2")]
+                 + [W(S[j], z, i, w) for z in O if j == 3 for i, w in ((2, "up1"), (3, "up2"))])
+        for j in (0, 2):
+            key = ["rW%d" % j, "rW%d" % (j + 1)]
+            for z in Y:
+                send(X, 4, key, [W(X, z, j, "off"), W(X, z, j + 1, "up")])
+            send(E, 5, key, [W(E, F, j, "lo"), W(E, F, j + 1, "hi")])
+            if M:
+                send(E2, 5, key, [W(E2, F2, j, "lo"), W(E2, F2, j + 1, "hi")])
+        for j, m in enumerate(M):
+            send(m, 3, "rFW", [FW(m, E2, j, "off")])
     order, back = {}, {}
     for o in range(n):
-        def key(k, o=o):
-            if k == o:
-                return 9
-            if H[k] == H[o]:
-                return 5
-            if o not in near[k]:
-                return 3
-            return 1 if C[k] == C[o] else 2
-        order[o] = sorted(range(n), key=key)
-        back[o] = [o] + [k for k in order[o] if H[k] == H[o] and k != o] + [k for k in order[o] if H[k] != H[o]]
-        for k in order[o][:-1]:
-            d = where[(k, o)]
-            hd = topo.host(d)
-            what = "up" if hd == H[o] else ("lo" if topo.rack(hd) != topo.rack(H[o]) else "hi")
-            send(R[o], "gx%d" % k, [(d, "tk", 0, 192, "gx", 192 * k, 192 * k + 192, "rTK", eng(R[o], d, what))])
+        lev = {1: [], 2: [], 3: []}
+        for k in range(n):
+            if k != o:
+                lev[3 if o not in near[k] else (1 if C[k] == C[o] else 2)].append(k)
+        lev[2].sort(key=lambda k: H[k] == H[o])
+        for ks in lev.values():
+            if not ks:
+                continue
+            own = [k for k in ks if topo.host(where[(k, o)]) == H[o]]
+            sw = [k for k in ks if k not in own]
+            what = dict(zip(own, ["up"] if len(own) == 1 else ["up1", "up2"]))
+            what.update(dict(zip(sw, ["off"] if len(sw) == 1 else ["lo", "hi"])))
+            send(R[o], 1, ["gx%d" % k for k in ks], [(where[(k, o)], "tk", 0, 192, "gx", 192 * k, 192 * k + 192, "rTK",
+                                                     eng(R[o], where[(k, o)], what[k])) for k in sw + own])
+        order[o] = [k for ks in lev.values() for k in ks] + [o]
+        back[o] = [o] + [k for k in order[o] if k != o]
     for (k, o), c in where.items():
         if c != R[o]:
-            send(c, "ot", [(R[o], "res", 192 * k, 192 * k + 192, "ot", 0, 192, "rRS%d" % k, eng(c, R[o], "all"))])
+            send(c, 9, "ot", [(R[o], "res", 192 * k, 192 * k + 192, "ot", 0, 192, "rRS%d" % k, eng(c, R[o], "all"))])
+    for c in sends:
+        sends[c] = [t[1:] for t in sorted(sends[c], key=lambda t: t[0])]
     return {"pair": pair, "sends": sends, "arr": arr, "order": order, "back": back}
 
 
@@ -232,17 +256,15 @@ def rank_program(g, core, T, topo):
 
     EQ, MUL, ADD, SUB, MAX = AluOpType.is_equal, AluOpType.mult, AluOpType.add, AluOpType.subtract, AluOpType.max
     compute = core in plan["pair"]
-    xgate = new()
-    if me is not None:
-        cnt[xgate] = 1
 
     if me is not None:
+        xgate = new()
+        cnt[xgate] = 1
         ld_pick = done(SY.dma_start(T.picki[0:RW, :], T.pick[:, :]), None, 16)
-        ld_w1 = done(SY.dma_start(T.wa[:, :], T.w1[:, :]), None, 16)
+        ld_gate = done(S.dma_start(T.gin[0:RW, :], T.gate[:, :]), None, 16)
         pg0 = done(V.memset(T.pg[:, :], 0.0))
-        wait(S, "s", [pg0])
-        ld_gate = done(S.dma_start(T.pg[0:RW, 8:14], T.gate[:, :]), None, 16)
-        ld_w2 = done(S.dma_start(T.wb[:, :], T.w2[:, :]), None, 16)
+        ld_w1 = done(SY.dma_start(T.ww[:, 0:512], T.w1[:, :]), None, 16)
+        ld_w2 = done(SY.dma_start(T.ww[:, 512:1024], T.w2[:, :]), None, 16)
         ld_x1 = done(SY.dma_start(T.xw[:, CAPP:CAPP + TOK // 2], T.x[:, 0:TOK // 2]), None, 16)
         wait(SY, "y", [xgate])
         ld_x2 = done(SY.dma_start(T.xw[:, CAPP + TOK // 2:WIN], T.x[:, TOK // 2:TOK]), None, 16)
@@ -270,7 +292,8 @@ def rank_program(g, core, T, topo):
         e_rk = done(pe([c_kc]).matmul(T.rk[0:RW, 0:36], T.onef[0:1, 0:RW], T.kc[0:1, :], True, False))
         e_own = done(vec([ld_pick]).tensor_scalar(T.own[0:RW, :], T.picki[0:RW, :], 11, None, AluOpType.arith_shift_right))
         e_pf = done(vec([pg0]).tensor_copy(T.pg[0:RW, 0:6], T.picki[0:RW, :]))
-        evs["pg"] = [e_pf, ld_gate]
+        done(vec([ld_gate]).tensor_copy(T.pg[0:RW, 6:12], T.gin[0:RW, :]), e_pf)
+        evs["pg"] = [e_pf]
         e_mk = None
         for o in range(6):
             e_mk = done(vec([e_own]).tensor_scalar(T.mk[0:RW, 6 * o:6 * o + 6], T.own[0:RW, :], float(o), None, EQ), e_mk)
@@ -280,9 +303,9 @@ def rank_program(g, core, T, topo):
         e_uw = done(vec([]).tensor_scalar(T.uw[0:RW, :], T.own[0:RW, :], float(CAPP - TOK), float(CAPP), MUL, ADD))
         e_uu = done(vec([e_uw]).tensor_tensor(T.uu[0:RW, :], T.uw[0:RW, :], T.picki[0:RW, :], ADD))
         e_sm = done(vec([e_rk]).tensor_tensor(T.sm[0:RW, :], T.rk[0:RW, 0:36], T.mk[0:RW, :], MUL))
-        e_s18 = done(vec([e_sm]).tensor_tensor(T.s18[0:RW, :], T.sm[0:RW, 0:18], T.sm[0:RW, 18:36], ADD))
-        e_s6 = done(vec([e_s18]).tensor_tensor(T.s6[0:RW, :], T.s18[0:RW, 0:6], T.s18[0:RW, 6:12], ADD))
-        e_sl = done(vec([e_s6]).tensor_tensor(T.slot[0:RW, :], T.s6[0:RW, :], T.s18[0:RW, 12:18], ADD))
+        e_sl = None
+        for c in range(CH):
+            e_sl = done(vec([e_sm]).tensor_reduce(T.slot[0:RW, c:c + 1], T.sm[0:RW, c:36:6], AxisListType.X, MAX), e_sl)
         e_hl = done(vec([e_sl]).tensor_scalar(T.hl[0:RW, 0:6], T.slot[0:RW, :], 4, None, AluOpType.arith_shift_right))
         done(V.tensor_scalar(T.hl[0:RW, 6:12], T.slot[0:RW, :], 15, None, AluOpType.bitwise_and), e_hl)
         e_vv = done(vec([e_uu]).tensor_tensor(T.vv[0:RW, :], T.uu[0:RW, :], T.slot[0:RW, :], SUB))
@@ -298,7 +321,7 @@ def rank_program(g, core, T, topo):
         evs["lt"] = [e_lt]
         done(V.memset(T.yw[:, WIN // 2:WIN], 0.0), y0)
 
-    def gate_first(k, o, deps):
+    def gate_rows(k, o, deps):
         a = done(vec(deps).tensor_scalar(T.ga[0:RW, :], T.pg[0:RW, 0:6], float(TOK * o), None, AluOpType.is_ge))
         done(V.tensor_scalar(T.gb[0:RW, :], T.pg[0:RW, 0:6], float(TOK * o + TOK), None, AluOpType.is_lt), a)
         b = done(vec([a]).tensor_tensor(T.gm[0:RW, :], T.ga[0:RW, :], T.gb[0:RW, :], MUL))
@@ -309,19 +332,19 @@ def rank_program(g, core, T, topo):
         t = done(vec([s]).tensor_tensor(T.gs[0:RW, 6:12], T.gs[0:RW, 0:6], T.gm[0:RW, :], MUL))
         u = done(vec([t]).tensor_scalar(T.gs[0:RW, 12:18], T.gs[0:RW, 6:12], 1.0, None, SUB))
         vec([u, c_it])
-        h = None
+        h, W = None, CAPP
         for c in range(CH):
-            h = done(V.tensor_scalar(T.ohg[0:RW, 192 * c:192 * c + 192], T.it[0:RW, :], T.gs[0:RW, 12 + c:13 + c],
-                                     T.pg[0:RW, 8 + c:9 + c], EQ, MUL), h)
-        m = None
-        for c in range(CH):
-            m = done(pe([h, c_onf]).matmul(T.gp[:, 0:192], T.onef[0:RW, :], T.ohg[0:RW, 192 * c:192 * c + 192],
-                                           c == 0, c == CH - 1), m)
-        return m
+            h = done(V.tensor_scalar(T.ohg[0:RW, W * c:W * c + W], T.it[0:RW, :], T.gs[0:RW, 12 + c:13 + c],
+                                     T.pg[0:RW, 6 + c:7 + c], EQ, MUL), h)
+        h = done(vec([h]).tensor_tensor(T.ohg[0:RW, 0:3 * W], T.ohg[0:RW, 0:3 * W], T.ohg[0:RW, 3 * W:6 * W], ADD))
+        h = done(vec([h]).tensor_tensor(T.ohg[0:RW, 0:W], T.ohg[0:RW, 0:W], T.ohg[0:RW, W:2 * W], ADD))
+        return done(vec([h]).tensor_tensor(T.ohg[0:RW, 0:W], T.ohg[0:RW, 0:W], T.ohg[0:RW, 2 * W:3 * W], ADD))
 
-    def layers(tok, tdeps, d1, d2, both):
+    def layers(tok, tdeps, wdeps, both, rows):
         H = [T.hp0, T.hp1, T.hp2, T.hp3]
-        a = [done(pe(tdeps + d1).matmul(H[f][:, 0:192], T.wa[:, 128 * f:128 * f + 128], tok, True, True)) for f in range(FF)]
+        a = [done(pe(tdeps + [wdeps[f // 2]]).matmul(H[f][:, 0:192], T.ww[:, 128 * f:128 * f + 128], tok, True, True))
+             for f in range(FF)]
+        gm = done(pe([rows, c_onf]).matmul(T.gp[:, 0:192], T.onef[0:RW, :], T.ohg[0:RW, 0:192], True, True))
         m = None
         for f in range(FF):
             hid = T.hid[:, 192 * f:192 * f + 192]
@@ -329,19 +352,19 @@ def rank_program(g, core, T, topo):
                 r = done(vec([a[f]]).tensor_scalar(hid, H[f][:, 0:192], 0.0, None, MAX))
             else:
                 r = done(sc([a[f]]).activation(hid, H[f][:, 0:192], ActivationFunctionType.Relu))
-            m = done(pe(d2 + [r]).matmul(T.op[:, 0:192], T.wb[:, 128 * f:128 * f + 128], hid, f == 0, f == FF - 1), m)
-        return m
+            m = done(pe([wdeps[2 + f // 2], r]).matmul(T.op[:, 0:192], T.ww[:, 512 + 128 * f:640 + 128 * f], hid,
+                                                       f == 0, f == FF - 1), m)
+        gt = done(vec([gm]).tensor_copy(T.gt[:, :], T.gp[:, 0:192]))
+        return done(vec([m, gt]).tensor_tensor(T.ot[:, :], T.op[:, 0:192], T.gt[:, :], MUL))
 
     if compute:
         k, o = plan["pair"][core]
     if compute and me is None:
-        gm = gate_first(k, o, ["rPG"])
-        gt = done(vec([gm]).tensor_copy(T.gt[:, :], T.gp[:, 0:192]))
-        m = layers(T.tk[:, :], ["rTK"], ["rP1"], ["rP2"], True)
-        evs["ot"] = [done(vec([m, gt]).tensor_tensor(T.ot[:, :], T.op[:, 0:192], T.gt[:, :], MUL))]
+        rows = gate_rows(k, o, [s for s in ("rG", "rGa", "rGb") if (core, s) in plan["arr"]])
+        evs["ot"] = [layers(T.tk[:, :], ["rTK"], ["rW0", "rW1", "rW2", "rW3"], True, rows)]
 
     if me is not None:
-        gm = gate_first(k, o, [e_pf, ld_gate])
+        rows = gate_rows(k, o, [e_pf])
         vec([x0, ld_x1, ld_x2])
 
         def off(k):
@@ -350,9 +373,7 @@ def rank_program(g, core, T, topo):
         for k in plan["order"][me]:
             dep = [e_lt] if k == me else ["rLS%d" % k]
             evs["gx%d" % k] = [done(vec(dep).tensor_copy(T.gx[:, 192 * k:192 * k + 192], T.xw[:, :].indirect(off(k))))]
-        gt = done(vec([gm]).tensor_copy(T.gt[:, :], T.gp[:, 0:192]))
-        m = layers(T.gx[:, 192 * me:192 * me + 192], evs["gx%d" % me], [ld_w1], [ld_w2], False)
-        last = done(vec([m, gt]).tensor_tensor(T.ot[:, :], T.op[:, 0:192], T.gt[:, :], MUL))
+        last = layers(T.gx[:, 192 * me:192 * me + 192], evs["gx%d" % me], [ld_w1, ld_w1, ld_w2, ld_w2], False, rows)
         last = done(vec([last, y0]).tensor_copy(T.yw[:, :].indirect(off(me)), T.ot[:, :]))
         for k in plan["back"][me][1:]:
             t = T.tmp[:, 192 * k:192 * k + 192]
@@ -365,7 +386,8 @@ def rank_program(g, core, T, topo):
 
     steps = plan["sends"][core]
     for i, (key, items) in enumerate(steps):
-        wait(g, "g", evs[key] if key in evs else [key])
+        for z in (key if isinstance(key, list) else [key]):
+            wait(g, "g", evs[z] if z in evs else [z])
         ev = new()
         cnt[ev] = sum(len(t[8]) for t in items)
         masks = [sum(1 << e for e in t[8]) for t in items]

from concourse.bass import DstId, RemoteDMATransfer
from concourse.mybir import AluOpType, AxisListType, ActivationFunctionType

TOK, FF, CAP, CAPP = 2048, 4, 576, 192
WIN = TOK + CAPP
RW, CH = 96, 6
LC = CAPP // 16
NEV = 120

SCRATCH = {
    "picki": ("sbuf", [128, 6], "int32"), "own": ("sbuf", [128, 6], "int32"), "slot": ("sbuf", [128, 6], "int32"),
    "hl": ("sbuf", [128, 12], "int32"), "hlf": ("sbuf", [128, 12], "float32"), "uu": ("sbuf", [128, 6], "float32"),
    "uw": ("sbuf", [128, 6], "float32"), "vv": ("sbuf", [128, 6], "float32"), "gin": ("sbuf", [128, 6], "float32"),
    "pg": ("sbuf", [128, 12], "float32"), "ww": ("sbuf", [128, 1024], "float32"), "fw": ("sbuf", [128, 256], "float32"),
    "lt": ("sbuf", [128, 72], "uint16"), "ls": ("sbuf", [128, 432], "uint16"),
    "mk": ("sbuf", [128, 36], "bfloat16"), "cu": ("sbuf", [128, 36], "bfloat16"), "seg": ("sbuf", [128, 36], "float32"),
    "segb": ("sbuf", [128, 36], "bfloat16"), "sm": ("sbuf", [128, 36], "float32"),
    "neg": ("sbuf", [128, 96], "bfloat16"), "tri": ("sbuf", [128, 96], "bfloat16"), "oneb": ("sbuf", [128, 96], "bfloat16"),
    "onef": ("sbuf", [128, 128], "float32"), "it": ("sbuf", [128, 192], "float32"), "im": ("sbuf", [128, 128], "float32"),
    "c16": ("sbuf", [128, 72], "float32"), "kc": ("sbuf", [128, 36], "float32"),
    "ohr": ("sbuf", [128, 432], "float32"), "ohl": ("sbuf", [128, 768], "float32"), "ohg": ("sbuf", [128, 1152], "float32"),
    "ga": ("sbuf", [128, 6], "float32"), "gb": ("sbuf", [128, 6], "float32"), "gm": ("sbuf", [128, 6], "bfloat16"),
    "gc6": ("sbuf", [128, 6], "bfloat16"), "gs": ("sbuf", [128, 18], "float32"), "gt": ("sbuf", [128, 192], "float32"),
    "xw": ("sbuf", [128, WIN], "float32"), "yw": ("sbuf", [128, WIN], "float32"),
    "gx": ("sbuf", [128, 1152], "float32"), "tk": ("sbuf", [128, 192], "float32"), "res": ("sbuf", [128, 1152], "float32"),
    "tmp": ("sbuf", [128, 1152], "float32"), "hid": ("sbuf", [128, 768], "float32"), "ot": ("sbuf", [128, 192], "float32"),
    "hp0": ("psum", [128, 512], "float32"), "hp1": ("psum", [128, 512], "float32"), "hp2": ("psum", [128, 512], "float32"),
    "hp3": ("psum", [128, 512], "float32"), "op": ("psum", [128, 512], "float32"), "gp": ("psum", [128, 512], "float32"),
    "rk": ("psum", [128, 512], "float32"), "lp": ("psum", [128, 512], "float32"),
}
SEMAPHORES = (["rG", "rGa", "rGb", "rW0", "rW1", "rW2", "rW3", "rFW", "rLT", "rTK"] + ["rLS%d" % k for k in range(6)]
              + ["rRS%d" % k for k in range(6)] + ["e%d" % i for i in range(NEV)])
PLAN = {}


def engines(mask):
    return [i for i in range(16) if (mask >> i) & 1]


def make_plan(T, topo):
    R = list(T.cores)
    n = len(R)
    H = [topo.host(c) for c in R]
    C = [topo.chip(c) for c in R]
    at = {}
    for c in range(512):
        at.setdefault((topo.host(c), topo.chip(c)), []).append(c)
    numbers = sorted(set(C))

    def other(ch):
        return [z for z in numbers if z != ch][0]

    def linked(a, b):
        return topo.may_write(at[(a, C[0])][0], at[(b, C[0])][0])

    def cabled(h):
        return [z for z in range(4) if topo.rack(z) != topo.rack(h) and linked(h, z)][0]

    def ports(h, ch):
        return [c for c in at[(h, ch)] if topo.may_write(c, at[(h, other(ch))][0])]

    def plain(h, ch):
        return [c for c in at[(h, ch)] if c not in ports(h, ch) and c not in R]

    rank_at = {(H[r], C[r]): r for r in range(n)}
    mid = [h for h in range(4) if h not in H][0]
    pair, where = {}, {}
    sends, arr = {}, {}

    def send(src, prio, key, items):
        for d, db, d0, d1, sb, s0, s1, sem, eng in items:
            arr[(d, sem)] = arr.get((d, sem), 0) + len(eng)
        sends.setdefault(src, []).append((prio, key, items))

    def eng(core, d, what):
        h, ch = topo.host(core), topo.chip(core)
        near_core = [c for c in at[(h, ch)] if c != core][0]
        same = [c for c in range(512) if topo.same_plane(core, c)][0]
        on, off = engines(topo.mask(core, near_core)), engines(topo.mask(core, same))
        up = [e for e in on if e not in off]
        a, b = len(off) // 2, len(off) // 4
        return {"off": off, "up": up, "lo": off[:a], "hi": off[a:], "lo1": off[:b], "lo2": off[b:a], "hi1": off[a:a + b],
                "hi2": off[a + b:], "up1": up[:len(up) // 2], "up2": up[len(up) // 2:], "all": engines(topo.mask(core, d))}[what]

    def G(src, d, what):
        return (d, "pg", 0, 12, "pg", 0, 12, "rG", eng(src, d, what))

    def Ga(src, d, what):
        return (d, "pg", 0, 6, "pg", 0, 6, "rGa", eng(src, d, what))

    def Gb(src, d, what):
        return (d, "pg", 6, 12, "pg", 6, 12, "rGb", eng(src, d, what))

    def W(src, d, j, what):
        return (d, "ww", 256 * j, 256 * j + 256, "ww", 256 * j, 256 * j + 256, "rW%d" % j, eng(src, d, what))

    def W_fw(src, d, j, what):
        return (d, "fw", 0, 256, "ww", 256 * j, 256 * j + 256, "rFW", eng(src, d, what))

    def FW(src, d, j, what):
        return (d, "ww", 256 * j, 256 * j + 256, "fw", 0, 256, "rW%d" % j, eng(src, d, what))

    def FW_fw(src, d, what):
        return (d, "fw", 0, 256, "fw", 0, 256, "rFW", eng(src, d, what))

    def LR(src, d, what):
        return (d, "lt", 0, 72, "lt", 0, 72, "rLT", eng(src, d, what))

    def LS(src, o, k, what):
        return (R[o], "ls", 72 * k, 72 * k + 72, "lt", 0, 72, "rLS%d" % k, eng(src, R[o], what))

    near = {k: [o for o in range(n) if H[o] == H[k] or linked(H[k], H[o])] for k in range(n)}
    for k in range(n):
        for o in range(n):
            h, ch = H[k], C[o]
            if h == H[o]:
                c = R[k] if C[k] == ch else plain(h, ch)[0]
            elif topo.rack(h) == topo.rack(H[o]):
                c = ports(h, ch)[1] if C[k] == ch else plain(h, ch)[1]
            else:
                t = H[o] if cabled(h) in H else cabled(h)
                c = ports(t, ch)[0] if C[k] == ch else plain(t, ch)[-1]
            pair[c] = (k, o)
            where[(k, o)] = c
    for k in range(n):
        h, ch, c0 = H[k], C[k], R[k]
        P, Q = ports(h, ch), plain(h, ch)
        L, S = P[2], [Q[0], P[1], Q[2], P[3]]
        same = [o for o in near[k] if C[o] == ch and o != k]
        cross = [o for o in near[k] if C[o] != ch]
        cross = [o for o in cross if H[o] != h] + [o for o in cross if H[o] == h]
        far = [o for o in range(n) if o not in near[k]]
        mate_o = [o for o in range(n) if H[o] != h and topo.rack(H[o]) == topo.rack(h)]
        X = where[(k, rank_at[(h, other(ch))])]
        Y = [where[(k, o)] for o in mate_o if C[o] != ch]
        O = [where[(k, o)] for o in mate_o if C[o] == ch]
        rest = [o for o in range(n) if topo.rack(H[o]) != topo.rack(h)]
        first = [o for o in rest if H[o] == cabled(h)] or rest
        E = where[(k, [o for o in first if C[o] == ch][0])]
        F = where[(k, [o for o in first if C[o] != ch][0])]
        M, E2, F2 = [], None, None
        PM, QM = ports(mid, ch), plain(mid, ch)
        if far and first != rest:
            M = [QM[0], PM[1], QM[-1], PM[3]]
            E2 = where[(k, [o for o in far if C[o] == ch][0])]
            F2 = where[(k, [o for o in far if C[o] != ch][0])]
        rl = (M[1] if M else PM[2]) if far else None
        it = [G(c0, L, "up1" if far and O else ("up" if far else "off"))]
        it += [G(c0, z, "up2" if far else "up") for z in O]
        it += [G(c0, rl, "off")] if far else []
        send(c0, 0, "pg", it)
        send(c0, 0, "w1", [W(c0, S[1], 0, "up1"), W(c0, S[1], 1, "up2"), W_fw(c0, S[0], 0, "hi")])
        send(c0, 0, "w2", [W(c0, S[3], 2, "up1"), W(c0, S[3], 3, "up2"), W_fw(c0, S[2], 2, "hi")])
        send(c0, 0, "lt", [LR(c0, L, "lo"), LR(c0, rl, "hi")] if far else [LR(c0, L, "off")])
        send(c0, 0, "lt", [LS(c0, o, k, w) for o, w in zip(same, ["off"] if len(same) == 1 else ["lo", "hi"])])
        if Y:
            send(L, 0, "rG", [Ga(L, X, "lo"), Gb(L, Y[0], "hi")])
            send(X, 0, "rGa", [Ga(X, Y[0], "all")])
            send(Y[0], 0, "rGb", [Gb(Y[0], X, "all")])
            if first != rest or not far:
                send(L, 0, "rG", [G(L, E, "off")])
        else:
            send(L, 0, "rG", [G(L, X, "lo"), G(L, E, "hi")])
        send(E, 0, "rG", [G(E, F, "off")])
        if far:
            z = E2 if M else E
            send(rl, 0, "rG", [G(rl, z, "all")])
            if M:
                send(E2, 0, "rG", [G(E2, F2, "off")])
        send(L, 1, "rLT", [LS(L, cross[0], k, "lo"), LS(L, cross[1], k, "hi")])
        if cross[2:]:
            send(L, 1, "rLT", [LS(L, cross[2], k, "off")])
        if far:
            send(rl, 1, "rLT", [LS(rl, far[0], k, "lo"), LS(rl, far[1], k, "hi")])
        for j in (0, 2):
            send(S[j], 2, "rFW", [FW(S[j], E, j, "lo"), FW_fw(S[j], M[j], "hi")] if M else [FW(S[j], E, j, "off")])
        for j in (1, 3):
            send(S[j], 2, "rW%d" % j, [W(S[j], E, j, "lo1"), W_fw(S[j], M[j], j, "lo2")] if M else [W(S[j], E, j, "lo")])
            send(S[j], 3, ["rW%d" % (j - 1), "rW%d" % j], [W(S[j], X, j - 1, "hi1"), W(S[j], X, j, "hi2")]
                 + [W(S[j], z, i, w) for z in O if j == 3 for i, w in ((2, "up1"), (3, "up2"))])
        for j in (0, 2):
            key = ["rW%d" % j, "rW%d" % (j + 1)]
            for z in Y:
                send(X, 4, key, [W(X, z, j, "off"), W(X, z, j + 1, "up")])
            send(E, 5, key, [W(E, F, j, "lo"), W(E, F, j + 1, "hi")])
            if M:
                send(E2, 5, key, [W(E2, F2, j, "lo"), W(E2, F2, j + 1, "hi")])
        for j, m in enumerate(M):
            send(m, 3, "rFW", [FW(m, E2, j, "off")])
    order, back = {}, {}
    for o in range(n):
        lev = {1: [], 2: [], 3: []}
        for k in range(n):
            if k != o:
                lev[3 if o not in near[k] else (1 if C[k] == C[o] else 2)].append(k)
        lev[2].sort(key=lambda k: H[k] == H[o])
        for ks in lev.values():
            if not ks:
                continue
            own = [k for k in ks if topo.host(where[(k, o)]) == H[o]]
            sw = [k for k in ks if k not in own]
            what = dict(zip(own, ["up"] if len(own) == 1 else ["up1", "up2"]))
            what.update(dict(zip(sw, ["off"] if len(sw) == 1 else ["lo", "hi"])))
            send(R[o], 1, ["gx%d" % k for k in ks], [(where[(k, o)], "tk", 0, 192, "gx", 192 * k, 192 * k + 192, "rTK",
                                                     eng(R[o], where[(k, o)], what[k])) for k in sw + own])
        order[o] = [k for ks in lev.values() for k in ks] + [o]
        back[o] = [o] + [k for k in order[o] if k != o]
    for (k, o), c in where.items():
        if c != R[o]:
            send(c, 9, "ot", [(R[o], "res", 192 * k, 192 * k + 192, "ot", 0, 192, "rRS%d" % k, eng(c, R[o], "all"))])
    for c in sends:
        sends[c] = [t[1:] for t in sorted(sends[c], key=lambda t: t[0])]
    return {"pair": pair, "sends": sends, "arr": arr, "order": order, "back": back}


def rank_program(g, core, T, topo):
    if "p" not in PLAN:
        PLAN["p"] = make_plan(T, topo)
    plan = PLAN["p"]
    if core not in plan["sends"]:
        return
    me = T.rank_of(core)
    V, PE, S, SY = g.vector, g.tensor, g.scalar, g.sync
    cnt, evs, waited, seen = {}, {}, set(), set()

    def new():
        name = "e%d" % len(cnt)
        cnt[name] = 0
        return name

    def wait(q, qn, deps):
        for d in deps:
            if d is None or (qn, d) in seen:
                continue
            seen.add((qn, d))
            waited.add(d)
            q.wait_ge(T.sem[d], cnt[d] if d in cnt else plan["arr"][(core, d)])

    def done(instr, ev=None, k=1):
        ev = ev or new()
        instr.then_inc(T.sem[ev], k)
        cnt[ev] += k
        return ev

    def vec(deps):
        wait(V, "v", deps)
        return V

    def pe(deps):
        wait(PE, "p", deps)
        return PE

    def sc(deps):
        wait(S, "s", deps)
        return S

    EQ, MUL, ADD, SUB, MAX = AluOpType.is_equal, AluOpType.mult, AluOpType.add, AluOpType.subtract, AluOpType.max
    compute = core in plan["pair"]

    if me is not None:
        xgate = new()
        cnt[xgate] = 1
        ld_pick = done(SY.dma_start(T.picki[0:RW, :], T.pick[:, :]), None, 16)
        ld_gate = done(S.dma_start(T.gin[0:RW, :], T.gate[:, :]), None, 16)
        pg0 = done(V.memset(T.pg[:, :], 0.0))
        ld_w1 = done(SY.dma_start(T.ww[:, 0:512], T.w1[:, :]), None, 16)
        ld_w2 = done(SY.dma_start(T.ww[:, 512:1024], T.w2[:, :]), None, 16)
        ld_x1 = done(SY.dma_start(T.xw[:, CAPP:CAPP + TOK // 2], T.x[:, 0:TOK // 2]), None, 16)
        wait(SY, "y", [xgate])
        ld_x2 = done(SY.dma_start(T.xw[:, CAPP + TOK // 2:WIN], T.x[:, TOK // 2:TOK]), None, 16)
        evs["w1"], evs["w2"] = [ld_w1], [ld_w2]

    if compute:
        c_neg = done(V.memset(T.neg[0:RW, :], -1.0))
        c_one = done(V.memset(T.oneb[0:RW, :], 1.0))
        c_onf = done(V.memset(T.onef[0:RW, :], 1.0))
        wait(g, "g", [c_neg])
        c_tri = done(g.affine_select(T.tri[0:RW, :], T.neg[0:RW, :], [[-1, RW]], AluOpType.is_ge, 0.0, 0, 1))
        if me is not None:
            c_seg = done(g.iota(T.seg[0:RW, :], [[0, 6], [1, 6]], 0, 0, allow_small_or_imprecise_dtypes=True))
            c_kc = done(g.iota(T.kc[0:1, :], [[CAPP, 6], [0, 6]], 0, 0, allow_small_or_imprecise_dtypes=True))
            c_im = done(g.iota(T.im[0:RW, :], [[0, 8], [1, 16]], 0, 0, allow_small_or_imprecise_dtypes=True))
            c_c16 = done(g.iota(T.c16[0:1, :], [[0, 6], [16, LC]], 0, 0, allow_small_or_imprecise_dtypes=True))
        c_it = done(g.iota(T.it[0:RW, :], [[1, CAPP]], 0, 0, allow_small_or_imprecise_dtypes=True))

    if me is not None:
        x0 = done(V.memset(T.xw[:, 0:CAPP], 0.0))
        y0 = done(V.memset(T.yw[:, 0:WIN // 2], 0.0))
        c_segb = done(vec([c_seg]).tensor_scalar(T.segb[0:RW, :], T.seg[0:RW, :], 1.0, None, AluOpType.min))
        e_lp = done(pe([c_onf, c_im, c_c16]).matmul(T.lp[:, 0:72], T.onef[0:1, :], T.c16[0:1, :], True, False))
        done(PE.matmul(T.lp[:, 0:72], T.im[0:1, :], T.onef[0:1, 0:72], False, False), e_lp)
        e_rk = done(pe([c_kc]).matmul(T.rk[0:RW, 0:36], T.onef[0:1, 0:RW], T.kc[0:1, :], True, False))
        e_own = done(vec([ld_pick]).tensor_scalar(T.own[0:RW, :], T.picki[0:RW, :], 11, None, AluOpType.arith_shift_right))
        e_pf = done(vec([pg0]).tensor_copy(T.pg[0:RW, 0:6], T.picki[0:RW, :]))
        done(vec([ld_gate]).tensor_copy(T.pg[0:RW, 6:12], T.gin[0:RW, :]), e_pf)
        evs["pg"] = [e_pf]
        e_mk = None
        for o in range(6):
            e_mk = done(vec([e_own]).tensor_scalar(T.mk[0:RW, 6 * o:6 * o + 6], T.own[0:RW, :], float(o), None, EQ), e_mk)
        done(pe([e_mk, c_tri]).matmul(T.rk[0:RW, 0:36], T.tri[0:RW, :], T.mk[0:RW, :], False, False), e_rk)
        e_cu = done(vec([e_mk, c_segb]).tensor_tensor_scan(T.cu[0:RW, :], T.segb[0:RW, :], T.mk[0:RW, :], 0.0, MUL, ADD))
        done(pe([e_cu, c_one]).matmul(T.rk[0:RW, 0:36], T.oneb[0:RW, :], T.cu[0:RW, :], False, True), e_rk)
        e_uw = done(vec([]).tensor_scalar(T.uw[0:RW, :], T.own[0:RW, :], float(CAPP - TOK), float(CAPP), MUL, ADD))
        e_uu = done(vec([e_uw]).tensor_tensor(T.uu[0:RW, :], T.uw[0:RW, :], T.picki[0:RW, :], ADD))
        e_sm = done(vec([e_rk]).tensor_tensor(T.sm[0:RW, :], T.rk[0:RW, 0:36], T.mk[0:RW, :], MUL))
        e_sl = None
        for c in range(CH):
            e_sl = done(vec([e_sm]).tensor_reduce(T.slot[0:RW, c:c + 1], T.sm[0:RW, c:36:6], AxisListType.X, MAX), e_sl)
        e_hl = done(vec([e_sl]).tensor_scalar(T.hl[0:RW, 0:6], T.slot[0:RW, :], 4, None, AluOpType.arith_shift_right))
        done(V.tensor_scalar(T.hl[0:RW, 6:12], T.slot[0:RW, :], 15, None, AluOpType.bitwise_and), e_hl)
        e_vv = done(vec([e_uu]).tensor_tensor(T.vv[0:RW, :], T.uu[0:RW, :], T.slot[0:RW, :], SUB))
        e_hf = done(vec([e_hl]).tensor_copy(T.hlf[0:RW, :], T.hl[0:RW, :]))
        vec([e_hf, e_vv, c_it, c_im])
        for c in range(CH):
            e_oh = done(V.tensor_scalar(T.ohr[0:RW, 72 * c:72 * c + 72], T.it[0:RW, 0:72], T.hlf[0:RW, c:c + 1],
                                        T.vv[0:RW, c:c + 1], EQ, MUL))
            done(V.tensor_scalar(T.ohl[0:RW, 128 * c:128 * c + 128], T.im[0:RW, :], T.hlf[0:RW, 6 + c:7 + c], None, EQ), e_oh)
            done(pe([e_oh]).matmul(T.lp[:, 0:72], T.ohl[0:RW, 128 * c:128 * c + 128], T.ohr[0:RW, 72 * c:72 * c + 72],
                                   False, c == CH - 1), e_lp)
        e_lt = done(vec([e_lp]).tensor_copy(T.lt[:, :], T.lp[:, 0:72]))
        evs["lt"] = [e_lt]
        done(V.memset(T.yw[:, WIN // 2:WIN], 0.0), y0)

    def gate_rows(k, o, deps):
        a = done(vec(deps).tensor_scalar(T.ga[0:RW, :], T.pg[0:RW, 0:6], float(TOK * o), None, AluOpType.is_ge))
        done(V.tensor_scalar(T.gb[0:RW, :], T.pg[0:RW, 0:6], float(TOK * o + TOK), None, AluOpType.is_lt), a)
        b = done(vec([a]).tensor_tensor(T.gm[0:RW, :], T.ga[0:RW, :], T.gb[0:RW, :], MUL))
        c = done(vec([b, c_one]).tensor_tensor_scan(T.gc6[0:RW, :], T.oneb[0:RW, 0:6], T.gm[0:RW, :], 0.0, MUL, ADD))
        r = done(pe([b, c_tri]).matmul(T.gp[0:RW, 0:6], T.tri[0:RW, :], T.gm[0:RW, :], True, False))
        done(pe([c, c_one]).matmul(T.gp[0:RW, 0:6], T.oneb[0:RW, :], T.gc6[0:RW, :], False, True), r)
        s = done(vec([r]).tensor_scalar(T.gs[0:RW, 0:6], T.gp[0:RW, 0:6], 1.0, None, ADD))
        t = done(vec([s]).tensor_tensor(T.gs[0:RW, 6:12], T.gs[0:RW, 0:6], T.gm[0:RW, :], MUL))
        u = done(vec([t]).tensor_scalar(T.gs[0:RW, 12:18], T.gs[0:RW, 6:12], 1.0, None, SUB))
        vec([u, c_it])
        h, W = None, CAPP
        for c in range(CH):
            h = done(V.tensor_scalar(T.ohg[0:RW, W * c:W * c + W], T.it[0:RW, :], T.gs[0:RW, 12 + c:13 + c],
                                     T.pg[0:RW, 6 + c:7 + c], EQ, MUL), h)
        h = done(vec([h]).tensor_tensor(T.ohg[0:RW, 0:3 * W], T.ohg[0:RW, 0:3 * W], T.ohg[0:RW, 3 * W:6 * W], ADD))
        h = done(vec([h]).tensor_tensor(T.ohg[0:RW, 0:W], T.ohg[0:RW, 0:W], T.ohg[0:RW, W:2 * W], ADD))
        return done(vec([h]).tensor_tensor(T.ohg[0:RW, 0:W], T.ohg[0:RW, 0:W], T.ohg[0:RW, 2 * W:3 * W], ADD))

    def layers(tok, tdeps, wdeps, both, rows):
        H = [T.hp0, T.hp1, T.hp2, T.hp3]
        a = [done(pe(tdeps + [wdeps[f // 2]]).matmul(H[f][:, 0:192], T.ww[:, 128 * f:128 * f + 128], tok, True, True))
             for f in range(FF)]
        gm = done(pe([rows, c_onf]).matmul(T.gp[:, 0:192], T.onef[0:RW, :], T.ohg[0:RW, 0:192], True, True))
        m = None
        for f in range(FF):
            hid = T.hid[:, 192 * f:192 * f + 192]
            if both and f % 2 == 0:
                r = done(vec([a[f]]).tensor_scalar(hid, H[f][:, 0:192], 0.0, None, MAX))
            else:
                r = done(sc([a[f]]).activation(hid, H[f][:, 0:192], ActivationFunctionType.Relu))
            m = done(pe([wdeps[2 + f // 2], r]).matmul(T.op[:, 0:192], T.ww[:, 512 + 128 * f:640 + 128 * f], hid,
                                                       f == 0, f == FF - 1), m)
        gt = done(vec([gm]).tensor_copy(T.gt[:, :], T.gp[:, 0:192]))
        return done(vec([m, gt]).tensor_tensor(T.ot[:, :], T.op[:, 0:192], T.gt[:, :], MUL))

    if compute:
        k, o = plan["pair"][core]
    if compute and me is None:
        rows = gate_rows(k, o, [s for s in ("rG", "rGa", "rGb") if (core, s) in plan["arr"]])
        evs["ot"] = [layers(T.tk[:, :], ["rTK"], ["rW0", "rW1", "rW2", "rW3"], True, rows)]

    if me is not None:
        rows = gate_rows(k, o, [e_pf])
        vec([x0, ld_x1, ld_x2])

        def off(k):
            return T.lt[:, LC * me:LC * me + LC] if k == me else T.ls[:, 72 * k + LC * me:72 * k + LC * me + LC]

        for k in plan["order"][me]:
            dep = [e_lt] if k == me else ["rLS%d" % k]
            evs["gx%d" % k] = [done(vec(dep).tensor_copy(T.gx[:, 192 * k:192 * k + 192], T.xw[:, :].indirect(off(k))))]
        last = layers(T.gx[:, 192 * me:192 * me + 192], evs["gx%d" % me], [ld_w1, ld_w1, ld_w2, ld_w2], False, rows)
        last = done(vec([last, y0]).tensor_copy(T.yw[:, :].indirect(off(me)), T.ot[:, :]))
        for k in plan["back"][me][1:]:
            t = T.tmp[:, 192 * k:192 * k + 192]
            a = done(vec(["rRS%d" % k, last]).tensor_tensor(t, T.yw[:, :].indirect(off(k)), T.res[:, 192 * k:192 * k + 192], ADD))
            last = done(vec([a]).tensor_copy(T.yw[:, :].indirect(off(k)), t))
        wait(SY, "y", [last])
        done(SY.dma_start(T.y[:, 0:TOK // 2], T.yw[:, CAPP:CAPP + TOK // 2]), None, 16)
        wait(S, "s", [last])
        done(S.dma_start(T.y[:, TOK // 2:TOK], T.yw[:, CAPP + TOK // 2:WIN]), None, 16)

    steps = plan["sends"][core]
    for i, (key, items) in enumerate(steps):
        for z in (key if isinstance(key, list) else [key]):
            wait(g, "g", evs[z] if z in evs else [z])
        ev = new()
        cnt[ev] = sum(len(t[8]) for t in items)
        masks = [sum(1 << e for e in t[8]) for t in items]
        if len(items) == 1:
            d, db, d0, d1, sb, s0, s1, sem, eng = items[0]
            rid, pid = topo.addr(d, core)
            g.remote_dma(T[db][:, d0:d1], T[sb][:, s0:s1], T.sem[sem], T.sem[ev], pid, rid, masks[0])
        else:
            tr = []
            for (d, db, d0, d1, sb, s0, s1, sem, eng), mk in zip(items, masks):
                rid, pid = topo.addr(d, core)
                tr.append(RemoteDMATransfer(dst_ids=[DstId(rid=rid, pnc=pid)], dma_engine_mask=mk, remote_sem=T.sem[sem],
                                            src=T[sb][:, s0:s1], dst=T[db][:, d0:d1]))
            g.remote_dma_fused(tr, local_sem=T.sem[ev])
        if me is not None and key == "lt" and steps[i + 1][0] != "lt":
            g.sem_inc(T.sem[xgate], 1)
    wait(g, "g", [e for e in cnt if e not in waited and cnt[e]])
    wait(g, "g", [s for (c, s) in plan["arr"] if c == core and s not in waited])
